import numpy as np
import ml_dtypes


def mxq(x, axis, fmt="e4m3"):
    dtype, down = {"e4m3": (ml_dtypes.float8_e4m3fn, 7), "e5m2": (ml_dtypes.float8_e5m2, 14)}[fmt]
    v = np.moveaxis(np.asarray(x, np.float32).astype(ml_dtypes.bfloat16).astype(np.float64), axis, -1)
    blocks = v.reshape(v.shape[:-1] + (-1, 32))
    amax = np.abs(blocks).max(-1, keepdims=True)
    byte = np.maximum(np.where(amax > 0, np.frexp(amax)[1] - 1 + 127, 0) - down, 1)
    scale = np.exp2(byte - 127.0)
    codes = (blocks / scale).astype(np.float32).astype(dtype).astype(np.float64)
    return np.moveaxis((codes * scale).reshape(v.shape), -1, axis)


WIDE = False


def mx_kscale(k):
    if not WIDE:
        return np.ones(k)
    levels = np.array([10, -10, 5, -5, 0])
    if k % 512:
        return np.exp2(np.random.permutation(np.resize(levels, k // 32))).repeat(32)
    a = np.empty((k // 512, 16))
    for p in range(k // 512):
        a[p, :8] = np.random.permutation(np.resize(levels, 8))
        for g in range(8):
            far = levels[np.abs(levels - a[p, g]) >= 10]
            a[p, g + 8] = far[np.random.randint(len(far))]
    return np.exp2(a.ravel()).repeat(32)


def f64(x):
    return np.asarray(x).astype(np.float64)


def striped(idx):
    return np.tile(idx.reshape(-1, 16).T, (8, 1)).astype(np.uint16)


def unstriped(offs):
    return offs[:16].T.reshape(-1).astype(np.int64)


K, T, E, C, N = 1536, 512, 4, 256, 512


def by_expert(wq, xq):
    return np.concatenate([wq[e].T @ xq[:, e * C:(e + 1) * C] for e in range(E)], axis=1)


def setup_inputs():
    n = np.random.standard_normal
    s = mx_kscale(K)[:, None]
    first = np.random.permutation(np.repeat(np.arange(E), T // E))
    second = (first + 1 + np.random.permutation(np.repeat(np.arange(E - 1), -(-T // (E - 1)))[:T])) % E
    while np.bincount(second, minlength=E).max() != T // E:
        load = np.bincount(second, minlength=E); hi, lo = int(load.argmax()), int(load.argmin())
        t = np.flatnonzero((second == hi) & (first != lo))[0]; second[t] = lo
    slot_token = np.empty(E * C, np.int64); pos = np.empty((2, T), np.int64); fill = np.zeros(E, np.int64)
    place = np.stack([np.random.permutation(C) for _ in range(E)])
    for r, deal in enumerate((first, second)):
        for t in np.random.permutation(T):
            e = deal[t]; j = e * C + place[e, fill[e]]; fill[e] += 1; slot_token[j] = t; pos[r, t] = j
    g = np.random.uniform(0.2, 0.8, T)
    return {
        "xT": (n((K, T)) * s).astype(np.float32),
        "w": (n((E, K, N)) / np.sqrt(K) / s[None]).astype(np.float32),
        "gate": np.stack([np.tile(g, (N, 1)), np.tile(1.0 - g, (N, 1))]).astype(np.float32),
        "offs": striped(slot_token),
        "pos1": striped(pos[0]),
        "pos2": striped(pos[1]),
    }


def reference(xT, w, gate, offs, pos1, pos2):
    idx = unstriped(offs)
    xq = mxq(f64(xT)[:, idx], 0, "e4m3")
    y = by_expert(mxq(f64(w), 1, "e4m3"), xq)
    return f64(gate[0]) * y[:, unstriped(pos1)] + f64(gate[1]) * y[:, unstriped(pos2)]

@@ -1,0 +1,148 @@
+from contextlib import ExitStack
+
+import concourse.mybir as mybir
+
+K, T, E, C, N = 1536, 512, 4, 256, 512
+FLOPS = 2 * K * N * E * C
+
+F32 = mybir.dt.float32
+BF16 = mybir.dt.bfloat16
+I32 = mybir.dt.int32
+U32 = mybir.dt.uint32
+U16 = mybir.dt.uint16
+U8 = mybir.dt.uint8
+FP8X4 = mybir.dt.float8_e4m3fn_x4
+MULT = mybir.AluOpType.mult
+ADD = mybir.AluOpType.add
+
+P = 128
+PACK = 4
+K_PASS = P * PACK
+PASSES = K // K_PASS
+BLOCKS = N // P
+SLOTS = E * C
+WINDOW = 1376
+XT_VECTOR = 256
+VSHARE = {3: 1, 11: 3}
+
+
+def interleave(copy, dst, src):
+    copy(out=dst.rearrange("p e (c i) t -> p e c t i", i=4), in_=src.rearrange("p e t (c i) -> p e c t i", i=4))
+
+
+def tile_routed_moe_kernel(tc, xT, w, gate, offs, pos1, pos2, out):
+    nc = tc.nc
+    with ExitStack() as ctx:
+        keep = ctx.enter_context(tc.tile_pool(name="keep", bufs=1))
+        xgp = ctx.enter_context(tc.tile_pool(name="xgp", bufs=2))
+        wgp = ctx.enter_context(tc.tile_pool(name="wgp", bufs=3))
+        wcp = ctx.enter_context(tc.tile_pool(name="wcp", bufs=5))
+        endp = ctx.enter_context(tc.tile_pool(name="endp", bufs=2))
+        psum = ctx.enter_context(tc.psum_pool(name="psum", bufs=1))
+
+        offs_t = keep.tile([P, SLOTS // 16], U16, name="offs_t")
+        pos1_t = keep.tile([P, T // 16], U16, name="pos1_t")
+        pos2_t = keep.tile([P, T // 16], U16, name="pos2_t")
+
+        x_words = [keep.tile([P, WINDOW], I32, name="x_words%d" % a, align_bytes=64) for a in range(PASSES)]
+        x_bytes = keep.tile([P, WINDOW], U8, name="x_bytes", align_bytes=64)
+        s_words = keep.tile([P, PASSES, SLOTS], U32, name="s_words", align_bytes=64)
+        s_bytes = keep.tile([P, SLOTS], U8, name="s_bytes", align_bytes=64)
+        nc.gpsimd.memset(x_bytes[:], 0)
+        for a in range(PASSES):
+            nc.vector.memset(x_words[a][:, T:], 0)
+
+        x_raw = []
+        for a in range(PASSES):
+            t = keep.tile([P, PACK, T], F32, name="x_raw%d" % a)
+            x_raw.append(t)
+            nc.sync.dma_start(out=t[:], in_=xT[a * K_PASS : (a + 1) * K_PASS, :].rearrange("(p j) n -> p j n", j=PACK))
+            if a == 0:
+                nc.sync.dma_start(offs_t[:], offs)
+
+        gates = [keep.tile([P, 2, T], F32, name="gate%d" % b) for b in range(BLOCKS)]
+
+        def load_gate(b):
+            if b == 0:
+                nc.sync.dma_start(pos1_t[:], pos1)
+                nc.sync.dma_start(pos2_t[:], pos2)
+            nc.sync.dma_start(out=gates[b][:], in_=gate[:, b * P : (b + 1) * P, :].rearrange("r p t -> p r t"))
+
+        w_raw = {}
+        for b in range(BLOCKS):
+            for a in range(PASSES):
+                t = keep.tile([P, E, PACK, P], F32, name="w_raw%d%d" % (b, a))
+                w_raw[b, a] = t
+                for e in range(E):
+                    nc.sync.dma_start(
+                        out=t[:, e, :, :],
+                        in_=w[e, a * K_PASS : (a + 1) * K_PASS, b * P : (b + 1) * P].rearrange("(p j) n -> p j n", j=PACK),
+                    )
+                if b > 0 and a == 0:
+                    load_gate(b - 1)
+        load_gate(BLOCKS - 1)
+
+        for a in range(PASSES):
+            grouped = xgp.tile([P, 1, T, PACK], BF16, name="x_grp", align_bytes=64)
+            raw = x_raw[a][:].rearrange("p (e t) n -> p e t n", e=1)
+            interleave(nc.vector.tensor_copy, grouped[:, :, :XT_VECTOR, :], raw[:, :, :, :XT_VECTOR])
+            interleave(nc.scalar.copy, grouped[:, :, XT_VECTOR:, :], raw[:, :, :, XT_VECTOR:])
+            nc.vector.quantize_mx(
+                out=x_words[a][:, :T].bitcast(FP8X4),
+                scales=x_bytes[4 * a :, :T],
+                in_=grouped[:].rearrange("p e w j -> p (e w j)"),
+            )
+        for a in range(PASSES):
+            nc.vector.tensor_copy(s_words[:, a, :], x_words[a][:].bitcast(U32).indirect(offs_t[:]))
+        nc.vector.tensor_copy(s_bytes[:], x_bytes[:].indirect(offs_t[:]))
+
+        sums = {}
+        banks = {}
+
+        def unit(b, a):
+            grouped = wgp.tile([P, E, P, PACK], BF16, name="w_grp", align_bytes=64)
+            v = VSHARE.get(b * PASSES + a, 0)
+            if v < E:
+                interleave(nc.scalar.copy, grouped[:, : E - v], w_raw[b, a][:, : E - v])
+            if v > 0:
+                interleave(nc.vector.tensor_copy, grouped[:, E - v :], w_raw[b, a][:, E - v :])
+            words = wcp.tile([P, E * P], U32, name="w_words", align_bytes=64)
+            byts = wcp.tile([P, E * P], U8, name="w_bytes", align_bytes=64)
+            nc.vector.quantize_mx(
+                out=words[:].bitcast(FP8X4), scales=byts[:], in_=grouped[:].rearrange("p e w j -> p (e w j)")
+            )
+            if a == 0:
+                sums[b] = endp.tile([P, SLOTS], F32, name="sums")
+            for e in range(E):
+                cols = slice(e * C, (e + 1) * C)
+                f = slice(e * P, (e + 1) * P)
+                if a == 0:
+                    banks[b, e] = psum.tile([P, C], F32, name="bank%d%d" % (b % 2, e))
+                nc.tensor.matmul_mx(
+                    out=banks[b, e][:],
+                    lhsT=words[:, f].bitcast(FP8X4),
+                    lhsT_scale=byts[:, f],
+                    rhs=s_words[:, a, cols].bitcast(FP8X4),
+                    rhs_scale=s_bytes[4 * a :, cols],
+                    start=(a == 0),
+                    stop=(a == PASSES - 1),
+                )
+                if a == PASSES - 1:
+                    copy = nc.vector.tensor_copy if b == BLOCKS - 1 and e % 2 == 1 else nc.scalar.copy
+                    copy(out=sums[b][:, cols], in_=banks[b, e][:])
+
+        def combine(b):
+            first = keep.tile([P, T], F32, name="first")
+            second = keep.tile([P, T], F32, name="second")
+            total = endp.tile([P, T], F32, name="total")
+            nc.vector.tensor_tensor(first[:], sums[b][:].indirect(pos1_t[:]), gates[b][:, 0, :], MULT)
+            nc.vector.tensor_tensor(second[:], sums[b][:].indirect(pos2_t[:]), gates[b][:, 1, :], MULT)
+            nc.vector.tensor_tensor(total[:], first[:], second[:], ADD)
+            nc.sync.dma_start(out=out[b * P : (b + 1) * P, :], in_=total[:])
+
+        for b in range(BLOCKS):
+            for a in range(PASSES):
+                unit(b, a)
+                if b > 0 and a == 0:
+                    combine(b - 1)
+        combine(BLOCKS - 1)

@@ -22,12 +22,21 @@ PASSES = K // K_PASS
 BLOCKS = N // P
 SLOTS = E * C
 WINDOW = 1376
-XT_VECTOR = 256
-VSHARE = {3: 1, 11: 3}
+XT_VECTOR = 288
+LOADS = (
+    [(e, a, 0, 512, 128) for e in range(3) for a in range(3)] + ["pos", 0]
+    + [(3, a, 0, 256, 128) for a in range(3)] + [1]
+    + [(3, a, 256, 256, 128) for a in range(3)] + [2, 3]
+)
+WORK = (
+    [(e, a, 0, 512, 128) for e in range(3) for a in range(3)]
+    + [(3, a, 0, 256, 64) for a in range(3)]
+    + [(3, 0, 256, 256, 64), 0, (3, 1, 256, 256, 64), 1, (3, 2, 256, 256, 128), 2, 3]
+)
 
 
 def interleave(copy, dst, src):
-    copy(out=dst.rearrange("p e (c i) t -> p e c t i", i=4), in_=src.rearrange("p e t (c i) -> p e c t i", i=4))
+    copy(out=dst.rearrange("p (c i) t -> p c t i", i=4), in_=src.rearrange("p t (c i) -> p c t i", i=4))
 
 
 def tile_routed_moe_kernel(tc, xT, w, gate, offs, pos1, pos2, out):
@@ -61,65 +70,61 @@ def tile_routed_moe_kernel(tc, xT, w, gate, offs, pos1, pos2, out):
                 nc.sync.dma_start(offs_t[:], offs)
 
         gates = [keep.tile([P, 2, T], F32, name="gate%d" % b) for b in range(BLOCKS)]
-
-        def load_gate(b):
-            if b == 0:
+        w_raw = {}
+        for item in LOADS:
+            if item == "pos":
                 nc.sync.dma_start(pos1_t[:], pos1)
                 nc.sync.dma_start(pos2_t[:], pos2)
-            nc.sync.dma_start(out=gates[b][:], in_=gate[:, b * P : (b + 1) * P, :].rearrange("r p t -> p r t"))
-
-        w_raw = {}
-        for b in range(BLOCKS):
-            for a in range(PASSES):
-                t = keep.tile([P, E, PACK, P], F32, name="w_raw%d%d" % (b, a))
-                w_raw[b, a] = t
-                for e in range(E):
-                    nc.sync.dma_start(
-                        out=t[:, e, :, :],
-                        in_=w[e, a * K_PASS : (a + 1) * K_PASS, b * P : (b + 1) * P].rearrange("(p j) n -> p j n", j=PACK),
-                    )
-                if b > 0 and a == 0:
-                    load_gate(b - 1)
-        load_gate(BLOCKS - 1)
+            elif isinstance(item, int):
+                b = item
+                nc.sync.dma_start(out=gates[b][:], in_=gate[:, b * P : (b + 1) * P, :].rearrange("r p t -> p r t"))
+            else:
+                e, a, n0, width, v = item
+                t = keep.tile([P, PACK, width], F32, name="w_raw%d_%d_%d" % (e, a, n0))
+                w_raw[e, a, n0] = t
+                nc.sync.dma_start(
+                    out=t[:],
+                    in_=w[e, a * K_PASS : (a + 1) * K_PASS, n0 : n0 + width].rearrange("(p j) n -> p j n", j=PACK),
+                )
 
         for a in range(PASSES):
-            grouped = xgp.tile([P, 1, T, PACK], BF16, name="x_grp", align_bytes=64)
-            raw = x_raw[a][:].rearrange("p (e t) n -> p e t n", e=1)
-            interleave(nc.vector.tensor_copy, grouped[:, :, :XT_VECTOR, :], raw[:, :, :, :XT_VECTOR])
-            interleave(nc.scalar.copy, grouped[:, :, XT_VECTOR:, :], raw[:, :, :, XT_VECTOR:])
+            grouped = xgp.tile([P, T, PACK], BF16, name="x_grp", align_bytes=64)
+            interleave(nc.vector.tensor_copy, grouped[:, :XT_VECTOR, :], x_raw[a][:, :, :XT_VECTOR])
+            interleave(nc.scalar.copy, grouped[:, XT_VECTOR:, :], x_raw[a][:, :, XT_VECTOR:])
             nc.vector.quantize_mx(
                 out=x_words[a][:, :T].bitcast(FP8X4),
                 scales=x_bytes[4 * a :, :T],
-                in_=grouped[:].rearrange("p e w j -> p (e w j)"),
+                in_=grouped[:].rearrange("p w j -> p (w j)"),
             )
         for a in range(PASSES):
             nc.vector.tensor_copy(s_words[:, a, :], x_words[a][:].bitcast(U32).indirect(offs_t[:]))
         nc.vector.tensor_copy(s_bytes[:], x_bytes[:].indirect(offs_t[:]))
 
-        sums = {}
         banks = {}
+        for b in range(BLOCKS):
+            for q in range(2):
+                banks[b, q] = psum.tile([P, 2 * C], F32, name="bank%d%d" % (b, q))
+        sums = [keep.tile([P, SLOTS], F32, name="sums%d" % b) for b in range(BLOCKS)]
 
-        def unit(b, a):
-            grouped = wgp.tile([P, E, P, PACK], BF16, name="w_grp", align_bytes=64)
-            v = VSHARE.get(b * PASSES + a, 0)
-            if v < E:
-                interleave(nc.scalar.copy, grouped[:, : E - v], w_raw[b, a][:, : E - v])
+        def unit(e, a, n0, width, v):
+            grouped = wgp.tile([P, width, PACK], BF16, name="w_grp", align_bytes=64)
+            raw = w_raw[e, a, n0]
+            if v < width:
+                interleave(nc.scalar.copy, grouped[:, v:, :], raw[:, :, v:])
             if v > 0:
-                interleave(nc.vector.tensor_copy, grouped[:, E - v :], w_raw[b, a][:, E - v :])
-            words = wcp.tile([P, E * P], U32, name="w_words", align_bytes=64)
-            byts = wcp.tile([P, E * P], U8, name="w_bytes", align_bytes=64)
+                interleave(nc.vector.tensor_copy, grouped[:, :v, :], raw[:, :, :v])
+            words = wcp.tile([P, width], U32, name="w_words", align_bytes=64)
+            byts = wcp.tile([P, width], U8, name="w_bytes", align_bytes=64)
             nc.vector.quantize_mx(
-                out=words[:].bitcast(FP8X4), scales=byts[:], in_=grouped[:].rearrange("p e w j -> p (e w j)")
+                out=words[:].bitcast(FP8X4), scales=byts[:], in_=grouped[:].rearrange("p w j -> p (w j)")
             )
-            if a == 0:
-                sums[b] = endp.tile([P, SLOTS], F32, name="sums")
-            for e in range(E):
-                cols = slice(e * C, (e + 1) * C)
-                f = slice(e * P, (e + 1) * P)
-                if a == 0:
-                    banks[b, e] = psum.tile([P, C], F32, name="bank%d%d" % (b % 2, e))
+            cols = slice(e * C, (e + 1) * C)
+            for i in range(width // P):
+                b = n0 // P + i
+                f = slice(i * P, (i + 1) * P)
+                bank = banks[b, e // 2][:, (e % 2) * C : (e % 2 + 1) * C]
                 nc.tensor.matmul_mx(
-                    out=banks[b, e][:],
+                    out=bank,
                     lhsT=words[:, f].bitcast(FP8X4),
                     lhsT_scale=byts[:, f],
                     rhs=s_words[:, a, cols].bitcast(FP8X4),
@@ -128,8 +133,8 @@ def tile_routed_moe_kernel(tc, xT, w, gate, offs, pos1, pos2, out):
                     stop=(a == PASSES - 1),
                 )
                 if a == PASSES - 1:
-                    copy = nc.vector.tensor_copy if b == BLOCKS - 1 and e % 2 == 1 else nc.scalar.copy
-                    copy(out=sums[b][:, cols], in_=banks[b, e][:])
+                    copy = nc.vector.tensor_copy if e == E - 1 and b % 2 == 1 else nc.scalar.copy
+                    copy(out=sums[b][:, cols], in_=bank)
 
         def combine(b):
             first = keep.tile([P, T], F32, name="first")
@@ -140,9 +145,8 @@ def tile_routed_moe_kernel(tc, xT, w, gate, offs, pos1, pos2, out):
             nc.vector.tensor_tensor(total[:], first[:], second[:], ADD)
             nc.sync.dma_start(out=out[b * P : (b + 1) * P, :], in_=total[:])
 
-        for b in range(BLOCKS):
-            for a in range(PASSES):
-                unit(b, a)
-                if b > 0 and a == 0:
-                    combine(b - 1)
-        combine(BLOCKS - 1)
+        for item in WORK:
+            if isinstance(item, int):
+                combine(item)
+            else:
+                unit(*item)

@@ -22,17 +22,13 @@ PASSES = K // K_PASS
 BLOCKS = N // P
 SLOTS = E * C
 WINDOW = 1376
-XT_VECTOR = 288
+XT_VECTOR = 128
 LOADS = (
-    [(e, a, 0, 512, 128) for e in range(3) for a in range(3)] + ["pos", 0]
-    + [(3, a, 0, 256, 128) for a in range(3)] + [1]
-    + [(3, a, 256, 256, 128) for a in range(3)] + [2, 3]
+    [(e, a, 0, 512, 0) for e in range(3) for a in range(3)] + [(3, 0, 0, 256, 0), "pos", (3, 1, 0, 256, 0), (3, 2, 0, 256, 0), 0]
+    + [(3, 0, 256, 256, 0), (3, 1, 256, 256, 0), 1, (3, 2, 256, 256, 0), 2, 3]
 )
-WORK = (
-    [(e, a, 0, 512, 128) for e in range(3) for a in range(3)]
-    + [(3, a, 0, 256, 64) for a in range(3)]
-    + [(3, 0, 256, 256, 64), 0, (3, 1, 256, 256, 64), 1, (3, 2, 256, 256, 128), 2, 3]
-)
+WORK = ([(e, a, 0, 512, 512 if (e, a) in ((1, 1), (2, 1)) else 0) for e in range(3) for a in range(3)] + [
+    (3, 0, 0, 256, 0), (3, 1, 0, 256, 256), (3, 2, 0, 256, 256), (3, 0, 256, 256, 0), (3, 1, 256, 256, 0), (3, 2, 256, 256, 0)] + [0, 1, 2, 3])
 
 
 def interleave(copy, dst, src):
@@ -43,9 +39,8 @@ def tile_routed_moe_kernel(tc, xT, w, gate, offs, pos1, pos2, out):
     nc = tc.nc
     with ExitStack() as ctx:
         keep = ctx.enter_context(tc.tile_pool(name="keep", bufs=1))
-        xgp = ctx.enter_context(tc.tile_pool(name="xgp", bufs=2))
-        wgp = ctx.enter_context(tc.tile_pool(name="wgp", bufs=3))
-        wcp = ctx.enter_context(tc.tile_pool(name="wcp", bufs=5))
+        rawp = ctx.enter_context(tc.tile_pool(name="rawp", bufs=9))
+        wgp = ctx.enter_context(tc.tile_pool(name="wgp", bufs=6))
         endp = ctx.enter_context(tc.tile_pool(name="endp", bufs=2))
         psum = ctx.enter_context(tc.psum_pool(name="psum", bufs=1))
 
@@ -63,7 +58,7 @@ def tile_routed_moe_kernel(tc, xT, w, gate, offs, pos1, pos2, out):
 
         x_raw = []
         for a in range(PASSES):
-            t = keep.tile([P, PACK, T], F32, name="x_raw%d" % a)
+            t = rawp.tile([P, PACK, T], F32, name="raw")
             x_raw.append(t)
             nc.sync.dma_start(out=t[:], in_=xT[a * K_PASS : (a + 1) * K_PASS, :].rearrange("(p j) n -> p j n", j=PACK))
             if a == 0:
@@ -80,7 +75,10 @@ def tile_routed_moe_kernel(tc, xT, w, gate, offs, pos1, pos2, out):
                 nc.sync.dma_start(out=gates[b][:], in_=gate[:, b * P : (b + 1) * P, :].rearrange("r p t -> p r t"))
             else:
                 e, a, n0, width, v = item
-                t = keep.tile([P, PACK, width], F32, name="w_raw%d_%d_%d" % (e, a, n0))
+                if width == N:
+                    t = rawp.tile([P, PACK, N], F32, name="raw")
+                else:
+                    t = keep.tile([P, PACK, width], F32, name="w_raw%d_%d_%d" % (e, a, n0))
                 w_raw[e, a, n0] = t
                 nc.sync.dma_start(
                     out=t[:],
@@ -88,7 +86,7 @@ def tile_routed_moe_kernel(tc, xT, w, gate, offs, pos1, pos2, out):
                 )
 
         for a in range(PASSES):
-            grouped = xgp.tile([P, T, PACK], BF16, name="x_grp", align_bytes=64)
+            grouped = wgp.tile([P, T, PACK], BF16, name="grouped", align_bytes=64)
             interleave(nc.vector.tensor_copy, grouped[:, :XT_VECTOR, :], x_raw[a][:, :, :XT_VECTOR])
             interleave(nc.scalar.copy, grouped[:, XT_VECTOR:, :], x_raw[a][:, :, XT_VECTOR:])
             nc.vector.quantize_mx(
@@ -107,14 +105,14 @@ def tile_routed_moe_kernel(tc, xT, w, gate, offs, pos1, pos2, out):
         sums = [keep.tile([P, SLOTS], F32, name="sums%d" % b) for b in range(BLOCKS)]
 
         def unit(e, a, n0, width, v):
-            grouped = wgp.tile([P, width, PACK], BF16, name="w_grp", align_bytes=64)
+            grouped = wgp.tile([P, width, PACK], BF16, name="grouped", align_bytes=64)
             raw = w_raw[e, a, n0]
             if v < width:
                 interleave(nc.scalar.copy, grouped[:, v:, :], raw[:, :, v:])
             if v > 0:
                 interleave(nc.vector.tensor_copy, grouped[:, :v, :], raw[:, :, :v])
-            words = wcp.tile([P, width], U32, name="w_words", align_bytes=64)
-            byts = wcp.tile([P, width], U8, name="w_bytes", align_bytes=64)
+            words = keep.tile([P, width], U32, name="w_words%d_%d_%d" % (e, a, n0), align_bytes=64)
+            byts = keep.tile([P, width], U8, name="w_bytes%d_%d_%d" % (e, a, n0), align_bytes=64)
             nc.vector.quantize_mx(
                 out=words[:].bitcast(FP8X4), scales=byts[:], in_=grouped[:].rearrange("p w j -> p (w j)")
             )
@@ -132,7 +130,9 @@ def tile_routed_moe_kernel(tc, xT, w, gate, offs, pos1, pos2, out):
                     start=(a == 0),
                     stop=(a == PASSES - 1),
                 )
-                if a == PASSES - 1:
+                if a == PASSES - 1 and e == 1:
+                    nc.scalar.copy(out=sums[b][:, : 2 * C], in_=banks[b, 0][:])
+                elif a == PASSES - 1 and e > 1:
                     copy = nc.vector.tensor_copy if e == E - 1 and b % 2 == 1 else nc.scalar.copy
                     copy(out=sums[b][:, cols], in_=bank)
 

@@ -23,12 +23,12 @@ BLOCKS = N // P
 SLOTS = E * C
 WINDOW = 1376
 XT_VECTOR = 128
-LOADS = (
-    [(e, a, 0, 512, 0) for e in range(3) for a in range(3)] + [(3, 0, 0, 256, 0), "pos", (3, 1, 0, 256, 0), (3, 2, 0, 256, 0), 0]
-    + [(3, 0, 256, 256, 0), (3, 1, 256, 256, 0), 1, (3, 2, 256, 256, 0), 2, 3]
-)
-WORK = ([(e, a, 0, 512, 512 if (e, a) in ((1, 1), (2, 1)) else 0) for e in range(3) for a in range(3)] + [
-    (3, 0, 0, 256, 0), (3, 1, 0, 256, 256), (3, 2, 0, 256, 256), (3, 0, 256, 256, 0), (3, 1, 256, 256, 0), (3, 2, 256, 256, 0)] + [0, 1, 2, 3])
+CHUNKS = [(e, a) for e in range(E) for a in range(PASSES)]
+LO = [(e, a, 0, 512) for e, a in CHUNKS[:8]] + [(e, a, 0, 256) for e, a in CHUNKS[8:]]
+HI = [(e, a, 256, 256) for e, a in CHUNKS[8:]]
+LOADS = LO + ["pos", 0] + HI[:-2] + [1] + HI[-2:] + [2, 3]
+VECTOR_UNITS = ((0, 2, 0), (2, 0, 0), (2, 1, 0), (3, 2, 0))
+WORK = LO + HI
 
 
 def interleave(copy, dst, src):
@@ -74,7 +74,7 @@ def tile_routed_moe_kernel(tc, xT, w, gate, offs, pos1, pos2, out):
                 b = item
                 nc.sync.dma_start(out=gates[b][:], in_=gate[:, b * P : (b + 1) * P, :].rearrange("r p t -> p r t"))
             else:
-                e, a, n0, width, v = item
+                e, a, n0, width = item
                 if width == N:
                     t = rawp.tile([P, PACK, N], F32, name="raw")
                 else:
@@ -104,13 +104,11 @@ def tile_routed_moe_kernel(tc, xT, w, gate, offs, pos1, pos2, out):
                 banks[b, q] = psum.tile([P, 2 * C], F32, name="bank%d%d" % (b, q))
         sums = [keep.tile([P, SLOTS], F32, name="sums%d" % b) for b in range(BLOCKS)]
 
-        def unit(e, a, n0, width, v):
+        def unit(e, a, n0, width):
             grouped = wgp.tile([P, width, PACK], BF16, name="grouped", align_bytes=64)
             raw = w_raw[e, a, n0]
-            if v < width:
-                interleave(nc.scalar.copy, grouped[:, v:, :], raw[:, :, v:])
-            if v > 0:
-                interleave(nc.vector.tensor_copy, grouped[:, :v, :], raw[:, :, :v])
+            copy = nc.vector.tensor_copy if (e, a, n0) in VECTOR_UNITS else nc.scalar.copy
+            interleave(copy, grouped[:], raw[:])
             words = keep.tile([P, width], U32, name="w_words%d_%d_%d" % (e, a, n0), align_bytes=64)
             byts = keep.tile([P, width], U8, name="w_bytes%d_%d_%d" % (e, a, n0), align_bytes=64)
             nc.vector.quantize_mx(
@@ -133,20 +131,25 @@ def tile_routed_moe_kernel(tc, xT, w, gate, offs, pos1, pos2, out):
                 if a == PASSES - 1 and e == 1:
                     nc.scalar.copy(out=sums[b][:, : 2 * C], in_=banks[b, 0][:])
                 elif a == PASSES - 1 and e > 1:
-                    copy = nc.vector.tensor_copy if e == E - 1 and b % 2 == 1 else nc.scalar.copy
-                    copy(out=sums[b][:, cols], in_=bank)
+                    nc.scalar.copy(out=sums[b][:, cols], in_=bank)
 
-        def combine(b):
-            first = keep.tile([P, T], F32, name="first")
-            second = keep.tile([P, T], F32, name="second")
+        products = {}
+
+        def product(b, r):
+            products[b, r] = endp.tile([P, T], F32, name="product%d" % r)
+            pos = (pos1_t, pos2_t)[r]
+            nc.vector.tensor_tensor(products[b, r][:], sums[b][:].indirect(pos[:]), gates[b][:, r, :], MULT)
+
+        def add_and_store(b):
             total = endp.tile([P, T], F32, name="total")
-            nc.vector.tensor_tensor(first[:], sums[b][:].indirect(pos1_t[:]), gates[b][:, 0, :], MULT)
-            nc.vector.tensor_tensor(second[:], sums[b][:].indirect(pos2_t[:]), gates[b][:, 1, :], MULT)
-            nc.vector.tensor_tensor(total[:], first[:], second[:], ADD)
+            nc.vector.tensor_tensor(total[:], products[b, 0][:], products[b, 1][:], ADD)
             nc.sync.dma_start(out=out[b * P : (b + 1) * P, :], in_=total[:])
 
         for item in WORK:
-            if isinstance(item, int):
-                combine(item)
-            else:
-                unit(*item)
+            unit(*item)
+        for b in range(BLOCKS):
+            product(b, 0)
+            if b > 0:
+                add_and_store(b - 1)
+            product(b, 1)
+        add_and_store(BLOCKS - 1)

@@ -22,12 +22,12 @@ PASSES = K // K_PASS
 BLOCKS = N // P
 SLOTS = E * C
 WINDOW = 1376
-XT_VECTOR = 128
+XT_VECTOR = 192
 CHUNKS = [(e, a) for e in range(E) for a in range(PASSES)]
 LO = [(e, a, 0, 512) for e, a in CHUNKS[:8]] + [(e, a, 0, 256) for e, a in CHUNKS[8:]]
-HI = [(e, a, 256, 256) for e, a in CHUNKS[8:]]
+HI = [(e, a, 256, 256) for e, a in CHUNKS[8:11]] + [(3, 2, 256, 128), (3, 2, 384, 128)]
 LOADS = LO + ["pos", 0] + HI[:-2] + [1] + HI[-2:] + [2, 3]
-VECTOR_UNITS = ((0, 2, 0), (2, 0, 0), (2, 1, 0), (3, 2, 0))
+VECTOR_UNITS = ((1, 1, 0), (2, 0, 0), (2, 1, 0), (3, 2, 0))
 WORK = LO + HI
 
 

from contextlib import ExitStack

import concourse.mybir as mybir

K, T, E, C, N = 1536, 512, 4, 256, 512
FLOPS = 2 * K * N * E * C

F32 = mybir.dt.float32
BF16 = mybir.dt.bfloat16
I32 = mybir.dt.int32
U32 = mybir.dt.uint32
U16 = mybir.dt.uint16
U8 = mybir.dt.uint8
FP8X4 = mybir.dt.float8_e4m3fn_x4
MULT = mybir.AluOpType.mult
ADD = mybir.AluOpType.add

P = 128
PACK = 4
K_PASS = P * PACK
PASSES = K // K_PASS
BLOCKS = N // P
SLOTS = E * C
WINDOW = 1376
XT_VECTOR = 192
CHUNKS = [(e, a) for e in range(E) for a in range(PASSES)]
LO = [(e, a, 0, 512) for e, a in CHUNKS[:8]] + [(e, a, 0, 256) for e, a in CHUNKS[8:]]
HI = [(e, a, 256, 256) for e, a in CHUNKS[8:11]] + [(3, 2, 256, 128), (3, 2, 384, 128)]
LOADS = LO + ["pos", 0] + HI[:-2] + [1] + HI[-2:] + [2, 3]
VECTOR_UNITS = ((1, 1, 0), (2, 0, 0), (2, 1, 0), (3, 2, 0))
WORK = LO + HI


def interleave(copy, dst, src):
    copy(out=dst.rearrange("p (c i) t -> p c t i", i=4), in_=src.rearrange("p t (c i) -> p c t i", i=4))


def tile_routed_moe_kernel(tc, xT, w, gate, offs, pos1, pos2, out):
    nc = tc.nc
    with ExitStack() as ctx:
        keep = ctx.enter_context(tc.tile_pool(name="keep", bufs=1))
        rawp = ctx.enter_context(tc.tile_pool(name="rawp", bufs=9))
        wgp = ctx.enter_context(tc.tile_pool(name="wgp", bufs=6))
        endp = ctx.enter_context(tc.tile_pool(name="endp", bufs=2))
        psum = ctx.enter_context(tc.psum_pool(name="psum", bufs=1))

        offs_t = keep.tile([P, SLOTS // 16], U16, name="offs_t")
        pos1_t = keep.tile([P, T // 16], U16, name="pos1_t")
        pos2_t = keep.tile([P, T // 16], U16, name="pos2_t")

        x_words = [keep.tile([P, WINDOW], I32, name="x_words%d" % a, align_bytes=64) for a in range(PASSES)]
        x_bytes = keep.tile([P, WINDOW], U8, name="x_bytes", align_bytes=64)
        s_words = keep.tile([P, PASSES, SLOTS], U32, name="s_words", align_bytes=64)
        s_bytes = keep.tile([P, SLOTS], U8, name="s_bytes", align_bytes=64)
        nc.gpsimd.memset(x_bytes[:], 0)
        for a in range(PASSES):
            nc.vector.memset(x_words[a][:, T:], 0)

        x_raw = []
        for a in range(PASSES):
            t = rawp.tile([P, PACK, T], F32, name="raw")
            x_raw.append(t)
            nc.sync.dma_start(out=t[:], in_=xT[a * K_PASS : (a + 1) * K_PASS, :].rearrange("(p j) n -> p j n", j=PACK))
            if a == 0:
                nc.sync.dma_start(offs_t[:], offs)

        gates = [keep.tile([P, 2, T], F32, name="gate%d" % b) for b in range(BLOCKS)]
        w_raw = {}
        for item in LOADS:
            if item == "pos":
                nc.sync.dma_start(pos1_t[:], pos1)
                nc.sync.dma_start(pos2_t[:], pos2)
            elif isinstance(item, int):
                b = item
                nc.sync.dma_start(out=gates[b][:], in_=gate[:, b * P : (b + 1) * P, :].rearrange("r p t -> p r t"))
            else:
                e, a, n0, width = item
                if width == N:
                    t = rawp.tile([P, PACK, N], F32, name="raw")
                else:
                    t = keep.tile([P, PACK, width], F32, name="w_raw%d_%d_%d" % (e, a, n0))
                w_raw[e, a, n0] = t
                nc.sync.dma_start(
                    out=t[:],
                    in_=w[e, a * K_PASS : (a + 1) * K_PASS, n0 : n0 + width].rearrange("(p j) n -> p j n", j=PACK),
                )

        for a in range(PASSES):
            grouped = wgp.tile([P, T, PACK], BF16, name="grouped", align_bytes=64)
            interleave(nc.vector.tensor_copy, grouped[:, :XT_VECTOR, :], x_raw[a][:, :, :XT_VECTOR])
            interleave(nc.scalar.copy, grouped[:, XT_VECTOR:, :], x_raw[a][:, :, XT_VECTOR:])
            nc.vector.quantize_mx(
                out=x_words[a][:, :T].bitcast(FP8X4),
                scales=x_bytes[4 * a :, :T],
                in_=grouped[:].rearrange("p w j -> p (w j)"),
            )
        for a in range(PASSES):
            nc.vector.tensor_copy(s_words[:, a, :], x_words[a][:].bitcast(U32).indirect(offs_t[:]))
        nc.vector.tensor_copy(s_bytes[:], x_bytes[:].indirect(offs_t[:]))

        banks = {}
        for b in range(BLOCKS):
            for q in range(2):
                banks[b, q] = psum.tile([P, 2 * C], F32, name="bank%d%d" % (b, q))
        sums = [keep.tile([P, SLOTS], F32, name="sums%d" % b) for b in range(BLOCKS)]

        def unit(e, a, n0, width):
            grouped = wgp.tile([P, width, PACK], BF16, name="grouped", align_bytes=64)
            raw = w_raw[e, a, n0]
            copy = nc.vector.tensor_copy if (e, a, n0) in VECTOR_UNITS else nc.scalar.copy
            interleave(copy, grouped[:], raw[:])
            words = keep.tile([P, width], U32, name="w_words%d_%d_%d" % (e, a, n0), align_bytes=64)
            byts = keep.tile([P, width], U8, name="w_bytes%d_%d_%d" % (e, a, n0), align_bytes=64)
            nc.vector.quantize_mx(
                out=words[:].bitcast(FP8X4), scales=byts[:], in_=grouped[:].rearrange("p w j -> p (w j)")
            )
            cols = slice(e * C, (e + 1) * C)
            for i in range(width // P):
                b = n0 // P + i
                f = slice(i * P, (i + 1) * P)
                bank = banks[b, e // 2][:, (e % 2) * C : (e % 2 + 1) * C]
                nc.tensor.matmul_mx(
                    out=bank,
                    lhsT=words[:, f].bitcast(FP8X4),
                    lhsT_scale=byts[:, f],
                    rhs=s_words[:, a, cols].bitcast(FP8X4),
                    rhs_scale=s_bytes[4 * a :, cols],
                    start=(a == 0),
                    stop=(a == PASSES - 1),
                )
                if a == PASSES - 1 and e == 1:
                    nc.scalar.copy(out=sums[b][:, : 2 * C], in_=banks[b, 0][:])
                elif a == PASSES - 1 and e > 1:
                    nc.scalar.copy(out=sums[b][:, cols], in_=bank)

        products = {}

        def product(b, r):
            products[b, r] = endp.tile([P, T], F32, name="product%d" % r)
            pos = (pos1_t, pos2_t)[r]
            nc.vector.tensor_tensor(products[b, r][:], sums[b][:].indirect(pos[:]), gates[b][:, r, :], MULT)

        def add_and_store(b):
            total = endp.tile([P, T], F32, name="total")
            nc.vector.tensor_tensor(total[:], products[b, 0][:], products[b, 1][:], ADD)
            nc.sync.dma_start(out=out[b * P : (b + 1) * P, :], in_=total[:])

        for item in WORK:
            unit(*item)
        for b in range(BLOCKS):
            product(b, 0)
            if b > 0:
                add_and_store(b - 1)
            product(b, 1)
        add_and_store(BLOCKS - 1)
